import numpy as np
CORES = [4,5,6,7,12,13,14,15,20,21,22,23,28,29,30,31]
N = 16
def setup_inputs(rng):
    return {"x1": rng.standard_normal((N, 128, 16), dtype=np.float32), "x2": rng.standard_normal((N, 128, 256), dtype=np.float32)}
def reference(x1, x2):
    out = []
    s = x1.sum(axis=0, dtype=np.float64).astype(x1.dtype)
    out.append(np.broadcast_to(s, (N,) + s.shape))
    out.append(np.broadcast_to(x2[8], x2.shape))
    return {"y1": out[0], "y2": out[1]}

@@ -1,0 +1,84 @@
+from concourse.bass import DstId, RemoteDMATransfer
+
+SCRATCH = {
+    "xa": ("sbuf", [128, 64], "float32"),
+    "pa": ("sbuf", [128, 64], "float32"),
+    "sa": ("sbuf", [128, 16], "float32"),
+    "b": ("sbuf", [128, 256], "float32"),
+}
+SEMAPHORES = ["ld1", "ld2", "gath", "part", "tot", "barr", "sent", "st1", "st2"]
+
+ROOT = 20
+TREE = {20: [21, 22, 23, 6], 22: [30], 6: [4, 5, 7, 14], 30: [28, 29, 31], 14: [12, 13, 15]}
+
+
+def rank_program(g, core, T, topo):
+    S = T.sem
+    chip, k = topo.chip(core), core % 8
+    base = chip * 8
+
+    def did(c):
+        rid, pid, _se = topo.addr(c)
+        return DstId(rid=rid, pnc=pid)
+
+    if k == 3:
+        g.wait_ge(S.gath, 4 * 8)
+        dsts = [8 * c + 2 for c in range(4)]
+        g.remote_dma_fused([RemoteDMATransfer(
+            dst_ids=[did(d) for d in dsts], dma_engine_mask=0x00FF, remote_sem=S.part,
+            srcs=[T.xa[:, 16 * j:16 * j + 16] for j in range(4)],
+            dsts=[T.pa[:, 16 * chip:16 * chip + 16] for d in dsts], alu_op=1)], local_sem=S.sent)
+        g.wait_ge(S.sent, 8)
+        return
+    if k == 2:
+        g.wait_ge(S.part, 4 * 8)
+        dsts = [base + 4 + j for j in range(4)]
+        g.remote_dma_fused([RemoteDMATransfer(
+            dst_ids=[did(d) for d in dsts], dma_engine_mask=0x00FF, remote_sem=S.tot,
+            srcs=[T.pa[:, 16 * j:16 * j + 16] for j in range(4)],
+            dsts=[T.sa[:] for d in dsts], alu_op=1)], local_sem=S.sent)
+        g.wait_ge(S.sent, 8)
+        return
+    if T.rank_of(core) is None:
+        return
+
+    j = k - 4
+    mine = T.xa[:, 16 * j:16 * j + 16]
+    g.sync.dma_start(mine, T.x1[:]).then_inc(S.ld1, 16)
+    if core == ROOT:
+        g.scalar.dma_start(T.b[:], T.x2[:]).then_inc(S.ld2, 16)
+
+    sent = 0
+    g.wait_ge(S.ld1, 16)
+    rid, pid, _se = topo.addr(base + 3)
+    g.remote_dma(mine, mine, remote_sem=S.gath, local_sem=S.sent, pid=pid, routing_id=rid, dma_engine_mask=0x00FF)
+    sent += 8
+
+    if core == ROOT:
+        g.wait_ge(S.ld2, 16)
+    elif core in TREE:
+        g.wait_ge(S.barr, 8)
+    if core in TREE:
+        near = [d for d in TREE[core] if topo.chip(d) == chip]
+        far = [d for d in TREE[core] if topo.chip(d) != chip]
+        tr = []
+        if near:
+            tr.append(RemoteDMATransfer(dst_ids=[did(d) for d in near], dma_engine_mask=0xFF00, remote_sem=S.barr,
+                                        srcs=[T.b[:]], dsts=[T.b[:] for d in near]))
+            sent += 8
+        if far:
+            tr.append(RemoteDMATransfer(dst_ids=[did(d) for d in far], dma_engine_mask=0x00FF, remote_sem=S.barr,
+                                        srcs=[T.b[:]], dsts=[T.b[:] for d in far]))
+            sent += 8
+        g.remote_dma_fused(tr, local_sem=S.sent)
+    g.wait_ge(S.sent, sent)
+
+    g.sync.wait_ge(S.tot, 8)
+    g.sync.dma_start(T.y1[:], T.sa[:]).then_inc(S.st1, 16)
+    g.sync.wait_ge(S.st1, 16)
+    if core == ROOT:
+        g.scalar.wait_ge(S.ld2, 16)
+    else:
+        g.scalar.wait_ge(S.barr, 8)
+    g.scalar.dma_start(T.y2[:], T.b[:]).then_inc(S.st2, 16)
+    g.scalar.wait_ge(S.st2, 16)

@@ -1,84 +1,105 @@
 from concourse.bass import DstId, RemoteDMATransfer
 
 SCRATCH = {
-    "xa": ("sbuf", [128, 64], "float32"),
-    "pa": ("sbuf", [128, 64], "float32"),
-    "sa": ("sbuf", [128, 16], "float32"),
-    "b": ("sbuf", [128, 256], "float32"),
+    "xa": ("dram", [4, 128, 16], "float32"),
+    "pa": ("dram", [4, 128, 16], "float32"),
+    "sa": ("dram", [128, 16], "float32"),
+    "bd": ("dram", [4, 128, 64], "float32"),
 }
-SEMAPHORES = ["ld1", "ld2", "gath", "part", "tot", "barr", "sent", "st1", "st2"]
+SEMAPHORES = ["ld1", "ld2", "gath", "part", "tot", "a0", "a1", "a2", "a3", "sent", "st1", "st2"]
 
 ROOT = 20
-TREE = {20: [21, 22, 23, 6], 22: [30], 6: [4, 5, 7, 14], 30: [28, 29, 31], 14: [12, 13, 15]}
+LOW, HIGH, ALL = 0x00FF, 0xFF00, 0xFFFF
+
+ROUTE = [
+    (20, 0, 0x000F, [6, 21]), (20, 1, 0x00F0, [2, 23]), (20, 2, 0x0F00, [22, 16]), (20, 3, 0xF000, [18]),
+    (6, 0, LOW, [12, 28]), (6, 0, HIGH, [4, 5, 7]),
+    (2, 1, LOW, [13, 29]), (2, 1, HIGH, [4, 5, 6, 7]),
+    (22, 2, LOW, [30, 14]), (22, 2, HIGH, [21, 23]),
+    (18, 3, LOW, [31, 15, 5]), (18, 3, HIGH, [21, 22, 23]),
+    (16, 2, LOW, [4]),
+    (21, 0, ALL, [22, 23]), (23, 1, ALL, [21, 22]),
+    (4, 2, ALL, [5, 6, 7]), (5, 3, ALL, [4, 6, 7]),
+]
+for _ch in (1, 3):
+    for _p in range(4):
+        ROUTE.append((8 * _ch + 4 + _p, _p, ALL, [8 * _ch + 4 + _j for _j in range(4) if _j != _p]))
+
+
+def engines(mask):
+    return bin(mask).count("1")
 
 
 def rank_program(g, core, T, topo):
     S = T.sem
     chip, k = topo.chip(core), core % 8
-    base = chip * 8
+    base = 8 * chip
+    arr = [S.a0, S.a1, S.a2, S.a3]
 
     def did(c):
         rid, pid, _se = topo.addr(c)
         return DstId(rid=rid, pnc=pid)
 
-    if k == 3:
-        g.wait_ge(S.gath, 4 * 8)
-        dsts = [8 * c + 2 for c in range(4)]
+    lands = {p: engines(m) for (_s, p, m, ds) in ROUTE if core in ds}
+    mine = [r for r in ROUTE if r[0] == core]
+
+    def forward():
+        if not mine:
+            return 0
         g.remote_dma_fused([RemoteDMATransfer(
-            dst_ids=[did(d) for d in dsts], dma_engine_mask=0x00FF, remote_sem=S.part,
-            srcs=[T.xa[:, 16 * j:16 * j + 16] for j in range(4)],
-            dsts=[T.pa[:, 16 * chip:16 * chip + 16] for d in dsts], alu_op=1)], local_sem=S.sent)
+            dst_ids=[did(d) for d in ds], dma_engine_mask=m, remote_sem=arr[p],
+            srcs=[T.bd[p]], dsts=[T.bd[p] for _d in ds]) for (_s, p, m, ds) in mine], local_sem=S.sent)
+        return sum(engines(m) for (_s, _p, m, _ds) in mine)
+
+    if k == 3:
+        g.wait_ge(S.gath, 4 * 16)
+        dsts = [8 * c + 1 for c in range(4)]
+        g.remote_dma_fused([RemoteDMATransfer(
+            dst_ids=[did(d) for d in dsts], dma_engine_mask=LOW, remote_sem=S.part,
+            srcs=[T.xa[j] for j in range(4)], dsts=[T.pa[chip] for _d in dsts], alu_op=1)], local_sem=S.sent)
         g.wait_ge(S.sent, 8)
         return
-    if k == 2:
+    if k == 1:
         g.wait_ge(S.part, 4 * 8)
         dsts = [base + 4 + j for j in range(4)]
         g.remote_dma_fused([RemoteDMATransfer(
-            dst_ids=[did(d) for d in dsts], dma_engine_mask=0x00FF, remote_sem=S.tot,
-            srcs=[T.pa[:, 16 * j:16 * j + 16] for j in range(4)],
-            dsts=[T.sa[:] for d in dsts], alu_op=1)], local_sem=S.sent)
-        g.wait_ge(S.sent, 8)
+            dst_ids=[did(d) for d in dsts], dma_engine_mask=ALL, remote_sem=S.tot,
+            srcs=[T.pa[c] for c in range(4)], dsts=[T.sa[:] for _d in dsts], alu_op=1)], local_sem=S.sent)
+        g.wait_ge(S.sent, 16)
         return
     if T.rank_of(core) is None:
+        for p in lands:
+            g.wait_ge(arr[p], lands[p])
+        n = forward()
+        if n:
+            g.wait_ge(S.sent, n)
         return
 
     j = k - 4
-    mine = T.xa[:, 16 * j:16 * j + 16]
-    g.sync.dma_start(mine, T.x1[:]).then_inc(S.ld1, 16)
+    g.sync.dma_start(T.xa[j], T.x1[:]).then_inc(S.ld1, 16)
     if core == ROOT:
-        g.scalar.dma_start(T.b[:], T.x2[:]).then_inc(S.ld2, 16)
+        g.scalar.dma_start(T.bd[:], T.x2[:]).then_inc(S.ld2, 16)
 
-    sent = 0
     g.wait_ge(S.ld1, 16)
     rid, pid, _se = topo.addr(base + 3)
-    g.remote_dma(mine, mine, remote_sem=S.gath, local_sem=S.sent, pid=pid, routing_id=rid, dma_engine_mask=0x00FF)
-    sent += 8
-
+    g.remote_dma(T.xa[j], T.xa[j], remote_sem=S.gath, local_sem=S.sent, pid=pid, routing_id=rid, dma_engine_mask=ALL)
+    n = 16
     if core == ROOT:
         g.wait_ge(S.ld2, 16)
-    elif core in TREE:
-        g.wait_ge(S.barr, 8)
-    if core in TREE:
-        near = [d for d in TREE[core] if topo.chip(d) == chip]
-        far = [d for d in TREE[core] if topo.chip(d) != chip]
-        tr = []
-        if near:
-            tr.append(RemoteDMATransfer(dst_ids=[did(d) for d in near], dma_engine_mask=0xFF00, remote_sem=S.barr,
-                                        srcs=[T.b[:]], dsts=[T.b[:] for d in near]))
-            sent += 8
-        if far:
-            tr.append(RemoteDMATransfer(dst_ids=[did(d) for d in far], dma_engine_mask=0x00FF, remote_sem=S.barr,
-                                        srcs=[T.b[:]], dsts=[T.b[:] for d in far]))
-            sent += 8
-        g.remote_dma_fused(tr, local_sem=S.sent)
-    g.wait_ge(S.sent, sent)
+    elif mine:
+        p = mine[0][1]
+        g.wait_ge(arr[p], lands[p])
+    n += forward()
+    g.wait_ge(S.sent, n)
 
-    g.sync.wait_ge(S.tot, 8)
+    g.sync.wait_ge(S.tot, 16)
     g.sync.dma_start(T.y1[:], T.sa[:]).then_inc(S.st1, 16)
     g.sync.wait_ge(S.st1, 16)
+
     if core == ROOT:
-        g.scalar.wait_ge(S.ld2, 16)
+        g.scalar.dma_start(T.y2[:], T.x2[:]).then_inc(S.st2, 16)
     else:
-        g.scalar.wait_ge(S.barr, 8)
-    g.scalar.dma_start(T.y2[:], T.b[:]).then_inc(S.st2, 16)
+        for p in range(4):
+            g.scalar.wait_ge(arr[p], lands[p])
+        g.scalar.dma_start(T.y2[:], T.bd[:]).then_inc(S.st2, 16)
     g.scalar.wait_ge(S.st2, 16)

from concourse.bass import DstId, RemoteDMATransfer

SCRATCH = {
    "xa": ("dram", [4, 128, 16], "float32"),
    "pa": ("dram", [4, 128, 16], "float32"),
    "sa": ("dram", [128, 16], "float32"),
    "bd": ("dram", [4, 128, 64], "float32"),
}
SEMAPHORES = ["ld1", "ld2", "gath", "part", "tot", "a0", "a1", "a2", "a3", "sent", "st1", "st2"]

ROOT = 20
LOW, HIGH, ALL = 0x00FF, 0xFF00, 0xFFFF

ROUTE = [
    (20, 0, 0x000F, [6, 21]), (20, 1, 0x00F0, [2, 23]), (20, 2, 0x0F00, [22, 16]), (20, 3, 0xF000, [18]),
    (6, 0, LOW, [12, 28]), (6, 0, HIGH, [4, 5, 7]),
    (2, 1, LOW, [13, 29]), (2, 1, HIGH, [4, 5, 6, 7]),
    (22, 2, LOW, [30, 14]), (22, 2, HIGH, [21, 23]),
    (18, 3, LOW, [31, 15, 5]), (18, 3, HIGH, [21, 22, 23]),
    (16, 2, LOW, [4]),
    (21, 0, ALL, [22, 23]), (23, 1, ALL, [21, 22]),
    (4, 2, ALL, [5, 6, 7]), (5, 3, ALL, [4, 6, 7]),
]
for _ch in (1, 3):
    for _p in range(4):
        ROUTE.append((8 * _ch + 4 + _p, _p, ALL, [8 * _ch + 4 + _j for _j in range(4) if _j != _p]))


def engines(mask):
    return bin(mask).count("1")


def rank_program(g, core, T, topo):
    S = T.sem
    chip, k = topo.chip(core), core % 8
    base = 8 * chip
    arr = [S.a0, S.a1, S.a2, S.a3]

    def did(c):
        rid, pid, _se = topo.addr(c)
        return DstId(rid=rid, pnc=pid)

    lands = {p: engines(m) for (_s, p, m, ds) in ROUTE if core in ds}
    mine = [r for r in ROUTE if r[0] == core]

    def forward():
        if not mine:
            return 0
        g.remote_dma_fused([RemoteDMATransfer(
            dst_ids=[did(d) for d in ds], dma_engine_mask=m, remote_sem=arr[p],
            srcs=[T.bd[p]], dsts=[T.bd[p] for _d in ds]) for (_s, p, m, ds) in mine], local_sem=S.sent)
        return sum(engines(m) for (_s, _p, m, _ds) in mine)

    if k == 3:
        g.wait_ge(S.gath, 4 * 16)
        dsts = [8 * c + 1 for c in range(4)]
        g.remote_dma_fused([RemoteDMATransfer(
            dst_ids=[did(d) for d in dsts], dma_engine_mask=LOW, remote_sem=S.part,
            srcs=[T.xa[j] for j in range(4)], dsts=[T.pa[chip] for _d in dsts], alu_op=1)], local_sem=S.sent)
        g.wait_ge(S.sent, 8)
        return
    if k == 1:
        g.wait_ge(S.part, 4 * 8)
        dsts = [base + 4 + j for j in range(4)]
        g.remote_dma_fused([RemoteDMATransfer(
            dst_ids=[did(d) for d in dsts], dma_engine_mask=ALL, remote_sem=S.tot,
            srcs=[T.pa[c] for c in range(4)], dsts=[T.sa[:] for _d in dsts], alu_op=1)], local_sem=S.sent)
        g.wait_ge(S.sent, 16)
        return
    if T.rank_of(core) is None:
        for p in lands:
            g.wait_ge(arr[p], lands[p])
        n = forward()
        if n:
            g.wait_ge(S.sent, n)
        return

    j = k - 4
    g.sync.dma_start(T.xa[j], T.x1[:]).then_inc(S.ld1, 16)
    if core == ROOT:
        g.scalar.dma_start(T.bd[:], T.x2[:]).then_inc(S.ld2, 16)

    g.wait_ge(S.ld1, 16)
    rid, pid, _se = topo.addr(base + 3)
    g.remote_dma(T.xa[j], T.xa[j], remote_sem=S.gath, local_sem=S.sent, pid=pid, routing_id=rid, dma_engine_mask=ALL)
    n = 16
    if core == ROOT:
        g.wait_ge(S.ld2, 16)
    elif mine:
        p = mine[0][1]
        g.wait_ge(arr[p], lands[p])
    n += forward()
    g.wait_ge(S.sent, n)

    g.sync.wait_ge(S.tot, 16)
    g.sync.dma_start(T.y1[:], T.sa[:]).then_inc(S.st1, 16)
    g.sync.wait_ge(S.st1, 16)

    if core == ROOT:
        g.scalar.dma_start(T.y2[:], T.x2[:]).then_inc(S.st2, 16)
    else:
        for p in range(4):
            g.scalar.wait_ge(arr[p], lands[p])
        g.scalar.dma_start(T.y2[:], T.bd[:]).then_inc(S.st2, 16)
    g.scalar.wait_ge(S.st2, 16)
